import numpy as np
import ml_dtypes


def mxq(x, axis, fmt="e4m3"):
    dtype, down = {"e4m3": (ml_dtypes.float8_e4m3fn, 7), "e5m2": (ml_dtypes.float8_e5m2, 14)}[fmt]
    v = np.moveaxis(np.asarray(x, np.float32).astype(ml_dtypes.bfloat16).astype(np.float64), axis, -1)
    blocks = v.reshape(v.shape[:-1] + (-1, 32))
    amax = np.abs(blocks).max(-1, keepdims=True)
    byte = np.maximum(np.where(amax > 0, np.frexp(amax)[1] - 1 + 127, 0) - down, 1)
    scale = np.exp2(byte - 127.0)
    codes = (blocks / scale).astype(np.float32).astype(dtype).astype(np.float64)
    return np.moveaxis((codes * scale).reshape(v.shape), -1, axis)


WIDE = False


def mx_kscale(k):
    if not WIDE:
        return np.ones(k)
    levels = np.array([10, -10, 5, -5, 0])
    if k % 512:
        return np.exp2(np.random.permutation(np.resize(levels, k // 32))).repeat(32)
    a = np.empty((k // 512, 16))
    for p in range(k // 512):
        a[p, :8] = np.random.permutation(np.resize(levels, 8))
        for g in range(8):
            far = levels[np.abs(levels - a[p, g]) >= 10]
            a[p, g + 8] = far[np.random.randint(len(far))]
    return np.exp2(a.ravel()).repeat(32)


def f64(x):
    return np.asarray(x).astype(np.float64)


def striped(idx):
    return np.tile(idx.reshape(-1, 16).T, (8, 1)).astype(np.uint16)


def unstriped(offs):
    return offs[:16].T.reshape(-1).astype(np.int64)


def silu(v):
    return v / (1.0 + np.exp(-np.maximum(v, -700.0)))


K, T, E, C, H, N = 1024, 768, 9, 256, 512, 128
TOP = 3


def by_expert(wq, xq):
    return np.concatenate([wq[e].T @ xq[:, e * C:(e + 1) * C] for e in range(E)], axis=1)


def setup_inputs():
    n = np.random.standard_normal
    s = mx_kscale(K)[:, None]
    u = mx_kscale(H)
    deal = np.repeat(np.arange(E), C).reshape(TOP, T)[:, np.random.permutation(T)]
    deal = np.take_along_axis(deal, np.argsort(np.random.rand(TOP, T), axis=0), axis=0)
    for _ in range(8):
        s_, t_ = np.random.permutation(T).reshape(2, -1); r = np.random.randint(TOP, size=T // 2); x, y = deal[r, s_].copy(), deal[r, t_].copy()
        ok = ~((deal[:, s_] == y).any(0) | (deal[:, t_] == x).any(0)); deal[r[ok], s_[ok]] = y[ok]; deal[r[ok], t_[ok]] = x[ok]
    order = np.lexsort((np.random.rand(TOP * T), deal.reshape(-1)))
    slot_token = order % T; pos = np.empty(TOP * T, np.int64); pos[order] = np.arange(TOP * T); pos = pos.reshape(TOP, T)
    g = np.random.uniform(0.5, 1.5, (TOP, T)); g = g / g.sum(0)
    w_slot = np.empty(E * C)
    for r in range(TOP): w_slot[pos[r]] = g[r]
    return {
        "xT": (n((K, T)) * s).astype(np.float32),
        "w1": (n((E, K, H)) / np.sqrt(K) / s[None] * u[None, None, :]).astype(np.float32),
        "w2": (n((E, H, N)) / np.sqrt(H) / u[None, :, None]).astype(np.float32),
        "gate": np.tile(w_slot, (K, 1)).astype(np.float32),
        "offs": striped(slot_token),
        "pos1": striped(pos[0]),
        "pos2": striped(pos[1]),
        "pos3": striped(pos[2]),
    }


def reference(xT, w1, w2, gate, offs, pos1, pos2, pos3):
    idx = unstriped(offs)
    xq = mxq(f64(gate) * f64(xT)[:, idx], 0, "e4m3")
    h = silu(by_expert(mxq(f64(w1), 1, "e4m3"), xq))
    y = by_expert(mxq(f64(w2), 1, "e4m3"), mxq(h, 0, "e4m3"))
    return y[:, unstriped(pos1)] + y[:, unstriped(pos2)] + y[:, unstriped(pos3)]

@@ -1,0 +1,217 @@
+from contextlib import ExitStack
+
+import concourse.mybir as mybir
+
+K, T, E, C, H, N = 1024, 768, 9, 256, 512, 128
+S = E * C
+FLOPS = 2 * S * (K * H + H * N)
+BYTES = 4 * (K * T + E * K * H + E * H * N + S + N * T) + 2 * 128 * (S + 3 * T) // 16
+
+F32 = mybir.dt.float32
+BF16 = mybir.dt.bfloat16
+U32 = mybir.dt.uint32
+U16 = mybir.dt.uint16
+U8 = mybir.dt.uint8
+FP8X4 = mybir.dt.float8_e4m3fn_x4
+MULT = mybir.AluOpType.mult
+ADD = mybir.AluOpType.add
+SILU = mybir.ActivationFunctionType.Silu
+
+P = 128
+PACK = 4
+PASSES = K // (P * PACK)
+HALF = 128
+SPARE = 16
+BATCHES = [(0, 3), (3, 3), (6, 2), (8, 1)]
+W2_GROUPS = [(0, 4), (4, 4), (8, 1)]
+VECTOR_CASTS_FROM = 8
+PIECES = [[(0, 384), (384, 384)], [(0, 384), (384, 384)], [(0, 384), (384, 256), (640, 128)]]
+
+
+def tile_moe_pre_mlp_silu_kernel(tc, xT, w1, w2, gate, offs, pos1, pos2, pos3, out):
+    nc = tc.nc
+    with ExitStack() as ctx:
+        keep = ctx.enter_context(tc.tile_pool(name="keep", bufs=1))
+        ring = ctx.enter_context(tc.tile_pool(name="ring", bufs=2))
+        psum = ctx.enter_context(tc.psum_pool(name="psum", bufs=2))
+
+        offs_sb = keep.tile([P, S // 16], U16, name="offs_sb")
+        pos_sb = [keep.tile([P, T // 16], U16, name="pos%d_sb" % r) for r in range(3)]
+        planes = {(g, j): keep.tile([P, T + SPARE], F32, name="plane%d%d" % (g, j)) for g in range(PASSES) for j in range(PACK)}
+        first = BATCHES[0][1] * C
+        gate_first = keep.tile([P, first], F32, name="gate_first")
+        gate_rest = keep.tile([P, S - first], F32, name="gate_rest")
+        y_sb = keep.tile([P, S], F32, name="y_sb")
+        w2_codes = keep.tile([P, E * N], U32, name="w2_codes", align_bytes=64)
+        w2_scales = keep.tile([P, E * N], U8, name="w2_scales", align_bytes=64)
+
+        x_rows = xT.rearrange("(g p j) t -> g j p t", g=PASSES, j=PACK)
+        raw, gathered, x_bf, x_q, w_bf, w_q, h_bf, h_ps, h_q, w2_raw = {}, {}, {}, {}, {}, {}, {}, {}, {}, {}
+
+        def load_plane(g, j):
+            nc.sync.dma_start(out=planes[g, j][:, 0:T], in_=x_rows[g, j])
+
+        def load_w1(e, g):
+            raw[e, g] = ring.tile([P, PACK, H], F32, name="raw", tag="raw", bufs=6)
+            nc.sync.dma_start(out=raw[e, g][:], in_=w1[e, g * 512 : (g + 1) * 512, :].rearrange("(p j) h -> p j h", j=PACK))
+
+        def load_w2(e0, n):
+            w2_raw[e0] = ring.tile([P, n, PACK * N], F32, name="w2_raw", tag="raw", bufs=6)
+            nc.sync.dma_start(out=w2_raw[e0][:], in_=w2[e0 : e0 + n].rearrange("e (p j) n -> p e (j n)", j=PACK))
+
+        def gather(e0, n, g):
+            t = ring.tile([P, PACK, n * C], F32, name="gathered", tag="gathered", bufs=2, align_bytes=64)
+            cols = slice(e0 * C // 16, (e0 + n) * C // 16)
+            gates = gate_first[:] if e0 == 0 else gate_rest[:, e0 * C - first : (e0 + n) * C - first]
+            for j in range(PACK):
+                nc.vector.tensor_tensor(t[:, j, :], planes[g, j][:].indirect(offs_sb[:, cols]), gates, MULT)
+            gathered[e0, g] = t
+
+        def cast_x(e0, n, g):
+            for i in range(n):
+                e = e0 + i
+                if g == 0:
+                    x_bf[e] = ring.tile([P, PASSES, C * PACK], BF16, name="x_bf", tag="x_bf", bufs=4, align_bytes=64)
+                nc.scalar.copy(
+                    x_bf[e][:, g, :].rearrange("p (c i j) -> p c j i", i=2, j=PACK),
+                    gathered[e0, g][:, :, i * C : (i + 1) * C].rearrange("p j (c i) -> p c j i", i=2),
+                )
+
+        def quantize(name, src, width, bufs):
+            codes = ring.tile([P, width], U32, name=name + "_codes", tag=name + "_codes", bufs=bufs, align_bytes=64)
+            scales = ring.tile([P, width], U8, name=name + "_scales", tag=name + "_scales", bufs=bufs, align_bytes=64)
+            nc.vector.quantize_mx(out=codes[:].bitcast(FP8X4), scales=scales[:], in_=src)
+            return codes, scales
+
+        def quantize_x(e):
+            x_q[e] = quantize("x", x_bf[e][:].rearrange("p g c -> p (g c)"), PASSES * C, 4)
+
+        def cast_w1(e, g):
+            src = raw[e, g][:].rearrange("p j (m t) -> p m j t", t=PACK)
+            if e < VECTOR_CASTS_FROM:
+                if g == 0:
+                    w_bf[e] = ring.tile([P, PASSES, PACK * H], BF16, name="w_bf", tag="w_bf", bufs=3, align_bytes=64)
+                w_bf[e, g] = w_bf[e][:, g, :]
+                nc.scalar.copy(w_bf[e, g].rearrange("p (t m j) -> p m j t", t=PACK, j=PACK), src)
+            else:
+                if g == 0:
+                    w_bf[e] = ring.tile([P, PASSES, PACK * H], BF16, name="w_bf_late", tag="gathered", bufs=2, align_bytes=64)
+                w_bf[e, g] = w_bf[e][:, g, :]
+                nc.vector.tensor_copy(w_bf[e, g].rearrange("p (t m j) -> p m j t", t=PACK, j=PACK), src)
+
+        def quantize_w1(e):
+            w_q[e] = quantize("w", w_bf[e][:].rearrange("p g c -> p (g c)"), PASSES * H, 4)
+
+        def prepare_w1(e):
+            for g in range(PASSES):
+                cast_w1(e, g)
+            quantize_w1(e)
+
+        def prepare_w2(e0, n):
+            t = ring.tile([P, n * N * PACK], BF16, name="w2_bf", tag="w_bf", bufs=3, align_bytes=64)
+            nc.vector.tensor_copy(
+                t[:].rearrange("p (e c i j) -> p e c j i", e=n, i=2, j=PACK),
+                w2_raw[e0][:].rearrange("p e (j c i) -> p e c j i", i=2, j=PACK),
+            )
+            cols = slice(e0 * N, (e0 + n) * N)
+            nc.vector.quantize_mx(out=w2_codes[:, cols].bitcast(FP8X4), scales=w2_scales[:, cols], in_=t[:])
+
+        def layer1(e):
+            h_bf[e] = ring.tile([P, C * PACK], BF16, name="h_bf", tag="h_bf", bufs=2, align_bytes=64)
+            for half in range(C // HALF):
+                ps = psum.tile([P, PACK, HALF], F32, name="a_ps", tag="a_ps", bufs=6)
+                for t in range(PACK):
+                    for g in range(PASSES):
+                        wc, ws = w_q[e]
+                        xc, xs = x_q[e]
+                        m = slice(g * H + t * P, g * H + (t + 1) * P)
+                        n = slice(g * C + half * HALF, g * C + (half + 1) * HALF)
+                        nc.tensor.matmul_mx(
+                            out=ps[:, t, :], lhsT=wc[:, m].bitcast(FP8X4), lhsT_scale=ws[:, m],
+                            rhs=xc[:, n].bitcast(FP8X4), rhs_scale=xs[:, n], start=(g == 0), stop=(g == PASSES - 1),
+                        )
+                nc.scalar.activation(
+                    h_bf[e][:, half * 512 : (half + 1) * 512].rearrange("p (n t) -> p n t", t=PACK),
+                    ps[:].rearrange("p t n -> p n t"), SILU,
+                )
+
+        def layer2(e):
+            hc, hs = quantize("h", h_bf[e][:], C, 2)
+            ps = psum.tile([P, C], F32, name="y_ps", tag="y_ps", bufs=2)
+            m = slice(e * N, (e + 1) * N)
+            nc.tensor.matmul_mx(
+                out=ps[:], lhsT=w2_codes[:, m].bitcast(FP8X4), lhsT_scale=w2_scales[:, m],
+                rhs=hc[:].bitcast(FP8X4), rhs_scale=hs[:], start=True, stop=True,
+            )
+            if e < VECTOR_CASTS_FROM:
+                nc.scalar.copy(y_sb[:, e * C : (e + 1) * C], ps[:])
+            else:
+                nc.vector.tensor_copy(y_sb[:, e * C : (e + 1) * C], ps[:])
+
+        for key in planes:
+            nc.gpsimd.memset(planes[key][:, T : T + SPARE], 0.0)
+
+        nc.sync.dma_start(offs_sb[:], offs)
+        load_plane(0, 0)
+        nc.sync.dma_start(out=gate_first[:], in_=gate[0:P, 0:first])
+        load_plane(0, 1)
+        load_w1(0, 0)
+        load_plane(0, 2)
+        load_plane(0, 3)
+        load_w1(0, 1)
+        load_plane(1, 0)
+        load_plane(1, 1)
+        load_w1(1, 0)
+        load_plane(1, 2)
+        load_plane(1, 3)
+        load_w1(1, 1)
+        nc.sync.dma_start(out=gate_rest[:], in_=gate[0:P, first:S])
+        for r, pos in enumerate((pos1, pos2, pos3)):
+            nc.sync.dma_start(pos_sb[r][:], pos)
+
+        units = [(e0, n, g) for e0, n in BATCHES for g in range(PASSES)]
+
+        def finish(e):
+            layer1(e)
+            if e > 0:
+                layer2(e - 1)
+
+        gather(*units[0])
+        prepare_w1(0)
+        for u in range(len(units)):
+            e0, n, g = units[u]
+            cast_x(e0, n, g)
+            if g == PASSES - 1:
+                for e in range(e0, e0 + n):
+                    quantize_x(e)
+            if u + 1 < len(units):
+                gather(*units[u + 1])
+            e = u + 1
+            if e >= 2:
+                load_w1(e, 0)
+                load_w1(e, 1)
+            prepare_w1(e)
+            for e0w, nw in W2_GROUPS:
+                if e0w == u - 1:
+                    load_w2(e0w, nw)
+                    prepare_w2(e0w, nw)
+            if u == len(units) - 1:
+                load_w2(*W2_GROUPS[-1])
+                prepare_w2(*W2_GROUPS[-1])
+            if u >= 1:
+                finish(u - 1)
+        finish(E - 2)
+        finish(E - 1)
+        layer2(E - 1)
+
+        sums = [keep.tile([P, T], F32, name="sum%d" % r) for r in range(3)]
+        for r in range(3):
+            for i, (t0, n) in enumerate(PIECES[r]):
+                cols = slice(t0, t0 + n)
+                picked = y_sb[:].indirect(pos_sb[r][:, t0 // 16 : (t0 + n) // 16])
+                if r == 0:
+                    nc.vector.tensor_copy(sums[r][:, cols], picked)
+                else:
+                    nc.vector.tensor_tensor(sums[r][:, cols], picked, sums[r - 1][:, cols], ADD)
+                if r == 2:
+                    (nc.sync if i % 2 == 0 else nc.scalar).dma_start(out=out[:, cols], in_=sums[r][:, cols])

@@ -23,8 +23,27 @@ PASSES = K // (P * PACK)
 HALF = 128
 SPARE = 16
 BATCHES = [(0, 3), (3, 3), (6, 2), (8, 1)]
-W2_GROUPS = [(0, 4), (4, 4), (8, 1)]
-VECTOR_CASTS_FROM = 8
+LAG1 = 1
+LAG2 = 4
+W2_LOAD = 0
+W2_LEAD = 1
+REST_LOAD = 2
+VY = 8
+WB_BUFS = 4
+WQ_BUFS = 8
+G_BUFS = 2
+H_BUFS = 2
+XB_BUFS = 4
+XQ_BUFS = 4
+RAW_BUFS = 6
+LATE_TAG = "w_bf"
+W2_GROUPS = [(3, (2, 1), 0, False), (5, (2, 1), 3, False), (7, (2, 1), 6, True)]
+LAGH = 2
+HQ_BUFS = 6
+SPLIT = 1
+VSET = (13, 15, 17)
+GSPLIT = 0
+LATE_BUFS = 4
 PIECES = [[(0, 384), (384, 384)], [(0, 384), (384, 384)], [(0, 384), (384, 256), (640, 128)]]
 
 
@@ -45,33 +64,42 @@ def tile_moe_pre_mlp_silu_kernel(tc, xT, w1, w2, gate, offs, pos1, pos2, pos3, o
         w2_codes = keep.tile([P, E * N], U32, name="w2_codes", align_bytes=64)
         w2_scales = keep.tile([P, E * N], U8, name="w2_scales", align_bytes=64)
 
+        w2_raw = {}
         x_rows = xT.rearrange("(g p j) t -> g j p t", g=PASSES, j=PACK)
-        raw, gathered, x_bf, x_q, w_bf, w_q, h_bf, h_ps, h_q, w2_raw = {}, {}, {}, {}, {}, {}, {}, {}, {}, {}
+        raw, gathered, x_bf, x_q, w_bf, w_q, h_bf, h_ps, h_q = {}, {}, {}, {}, {}, {}, {}, {}, {}
 
         def load_plane(g, j):
             nc.sync.dma_start(out=planes[g, j][:, 0:T], in_=x_rows[g, j])
 
         def load_w1(e, g):
-            raw[e, g] = ring.tile([P, PACK, H], F32, name="raw", tag="raw", bufs=6)
+            raw[e, g] = ring.tile([P, PACK, H], F32, name="raw", tag="raw", bufs=RAW_BUFS)
             nc.sync.dma_start(out=raw[e, g][:], in_=w1[e, g * 512 : (g + 1) * 512, :].rearrange("(p j) h -> p j h", j=PACK))
 
         def load_w2(e0, n):
-            w2_raw[e0] = ring.tile([P, n, PACK * N], F32, name="w2_raw", tag="raw", bufs=6)
-            nc.sync.dma_start(out=w2_raw[e0][:], in_=w2[e0 : e0 + n].rearrange("e (p j) n -> p e (j n)", j=PACK))
+            w2_raw[e0] = ring.tile([P, PACK, n, N], F32, name="w2_raw", tag="raw", bufs=RAW_BUFS)
+            rows = w2.rearrange("e (m t v) n -> v t m e n", t=PACK, v=2)
+            for v in range(2):
+                for t in range(PACK):
+                    nc.sync.dma_start(out=w2_raw[e0][v:P:2, t, :, :], in_=rows[v, t, :, e0 : e0 + n, :])
 
         def gather(e0, n, g):
-            t = ring.tile([P, PACK, n * C], F32, name="gathered", tag="gathered", bufs=2, align_bytes=64)
+            t = ring.tile([P, PACK, n * C], F32, name="gathered", tag="gathered", bufs=G_BUFS, align_bytes=64)
             cols = slice(e0 * C // 16, (e0 + n) * C // 16)
             gates = gate_first[:] if e0 == 0 else gate_rest[:, e0 * C - first : (e0 + n) * C - first]
             for j in range(PACK):
-                nc.vector.tensor_tensor(t[:, j, :], planes[g, j][:].indirect(offs_sb[:, cols]), gates, MULT)
+                if (e0, g, j) == (0, 0, 0) and GSPLIT:
+                    for c0, c1 in ((0, C), (C, first)):
+                        nc.vector.tensor_tensor(
+                            t[:, j, c0:c1], planes[g, j][:].indirect(offs_sb[:, c0 // 16 : c1 // 16]), gate_first[:, c0:c1], MULT)
+                else:
+                    nc.vector.tensor_tensor(t[:, j, :], planes[g, j][:].indirect(offs_sb[:, cols]), gates, MULT)
             gathered[e0, g] = t
 
         def cast_x(e0, n, g):
             for i in range(n):
                 e = e0 + i
                 if g == 0:
-                    x_bf[e] = ring.tile([P, PASSES, C * PACK], BF16, name="x_bf", tag="x_bf", bufs=4, align_bytes=64)
+                    x_bf[e] = ring.tile([P, PASSES, C * PACK], BF16, name="x_bf", tag="x_bf", bufs=XB_BUFS, align_bytes=64)
                 nc.scalar.copy(
                     x_bf[e][:, g, :].rearrange("p (c i j) -> p c j i", i=2, j=PACK),
                     gathered[e0, g][:, :, i * C : (i + 1) * C].rearrange("p j (c i) -> p c j i", i=2),
@@ -84,47 +112,56 @@ def tile_moe_pre_mlp_silu_kernel(tc, xT, w1, w2, gate, offs, pos1, pos2, pos3, o
             return codes, scales
 
         def quantize_x(e):
-            x_q[e] = quantize("x", x_bf[e][:].rearrange("p g c -> p (g c)"), PASSES * C, 4)
+            x_q[e] = quantize("x", x_bf[e][:].rearrange("p g c -> p (g c)"), PASSES * C, XQ_BUFS)
 
         def cast_w1(e, g):
-            src = raw[e, g][:].rearrange("p j (m t) -> p m j t", t=PACK)
-            if e < VECTOR_CASTS_FROM:
-                if g == 0:
-                    w_bf[e] = ring.tile([P, PASSES, PACK * H], BF16, name="w_bf", tag="w_bf", bufs=3, align_bytes=64)
-                w_bf[e, g] = w_bf[e][:, g, :]
-                nc.scalar.copy(w_bf[e, g].rearrange("p (t m j) -> p m j t", t=PACK, j=PACK), src)
+            src = raw[e, g][:].rearrange("p j (m t v) -> p m t j v", t=PACK, v=2)
+            if 2 * e + g not in VSET:
+                t = ring.tile([P, PACK * H], BF16, name="w_bf", tag="w_bf", bufs=WB_BUFS, align_bytes=64)
+                w_bf[e, g] = t[:]
+                nc.scalar.copy(w_bf[e, g].rearrange("p (t m v j) -> p m t j v", t=PACK, v=2, j=PACK), src)
             else:
-                if g == 0:
-                    w_bf[e] = ring.tile([P, PASSES, PACK * H], BF16, name="w_bf_late", tag="gathered", bufs=2, align_bytes=64)
-                w_bf[e, g] = w_bf[e][:, g, :]
-                nc.vector.tensor_copy(w_bf[e, g].rearrange("p (t m j) -> p m j t", t=PACK, j=PACK), src)
+                t = ring.tile([P, PACK * H], BF16, name="w_bf_late", tag=LATE_TAG, bufs=LATE_BUFS, align_bytes=64)
+                w_bf[e, g] = t[:]
+                nc.vector.tensor_copy(w_bf[e, g].rearrange("p (t m v j) -> p m t j v", t=PACK, v=2, j=PACK), src)
 
-        def quantize_w1(e):
-            w_q[e] = quantize("w", w_bf[e][:].rearrange("p g c -> p (g c)"), PASSES * H, 4)
+        def quantize_w1(e, g):
+            w_q[e, g] = quantize("w", w_bf[e, g], H, WQ_BUFS)
 
         def prepare_w1(e):
             for g in range(PASSES):
                 cast_w1(e, g)
-            quantize_w1(e)
+            for g in range(PASSES):
+                quantize_w1(e, g)
 
-        def prepare_w2(e0, n):
-            t = ring.tile([P, n * N * PACK], BF16, name="w2_bf", tag="w_bf", bufs=3, align_bytes=64)
+        def prepare_w2(widths, e0, late):
+            n = sum(widths)
+            if late:
+                t = ring.tile([P, n * N * PACK], BF16, name="w2_bf", tag=LATE_TAG, bufs=LATE_BUFS, align_bytes=64)
+            else:
+                t = ring.tile([P, n * N * PACK], BF16, name="w2_bf", tag="w2_bf", bufs=1, align_bytes=64)
             nc.vector.tensor_copy(
-                t[:].rearrange("p (e c i j) -> p e c j i", e=n, i=2, j=PACK),
-                w2_raw[e0][:].rearrange("p e (j c i) -> p e c j i", i=2, j=PACK),
+                t[:].rearrange("p (c i j) -> p c j i", i=2, j=PACK),
+                w2_raw[e0][:].rearrange("p j e (c i) -> p (e c) j i", i=2),
             )
-            cols = slice(e0 * N, (e0 + n) * N)
-            nc.vector.quantize_mx(out=w2_codes[:, cols].bitcast(FP8X4), scales=w2_scales[:, cols], in_=t[:])
+            done = 0
+            for width in widths:
+                cols = slice((e0 + done) * N, (e0 + done + width) * N)
+                nc.vector.quantize_mx(
+                    out=w2_codes[:, cols].bitcast(FP8X4), scales=w2_scales[:, cols],
+                    in_=t[:, done * N * PACK : (done + width) * N * PACK],
+                )
+                done = done + width
 
         def layer1(e):
-            h_bf[e] = ring.tile([P, C * PACK], BF16, name="h_bf", tag="h_bf", bufs=2, align_bytes=64)
+            h_bf[e] = ring.tile([P, C * PACK], BF16, name="h_bf", tag="h_bf", bufs=H_BUFS, align_bytes=64)
             for half in range(C // HALF):
                 ps = psum.tile([P, PACK, HALF], F32, name="a_ps", tag="a_ps", bufs=6)
                 for t in range(PACK):
                     for g in range(PASSES):
-                        wc, ws = w_q[e]
+                        wc, ws = w_q[e, g]
                         xc, xs = x_q[e]
-                        m = slice(g * H + t * P, g * H + (t + 1) * P)
+                        m = slice(t * P, (t + 1) * P)
                         n = slice(g * C + half * HALF, g * C + (half + 1) * HALF)
                         nc.tensor.matmul_mx(
                             out=ps[:, t, :], lhsT=wc[:, m].bitcast(FP8X4), lhsT_scale=ws[:, m],
@@ -135,18 +172,26 @@ def tile_moe_pre_mlp_silu_kernel(tc, xT, w1, w2, gate, offs, pos1, pos2, pos3, o
                     ps[:].rearrange("p t n -> p n t"), SILU,
                 )
 
+        def parts(e):
+            return [(0, C)] if e < E - SPLIT else [(0, HALF), (HALF, HALF)]
+
+        def quantize_h(e):
+            for c0, n in parts(e):
+                h_q[e, c0] = quantize("h", h_bf[e][:, c0 * PACK : (c0 + n) * PACK], n, HQ_BUFS)
+
         def layer2(e):
-            hc, hs = quantize("h", h_bf[e][:], C, 2)
-            ps = psum.tile([P, C], F32, name="y_ps", tag="y_ps", bufs=2)
-            m = slice(e * N, (e + 1) * N)
-            nc.tensor.matmul_mx(
-                out=ps[:], lhsT=w2_codes[:, m].bitcast(FP8X4), lhsT_scale=w2_scales[:, m],
-                rhs=hc[:].bitcast(FP8X4), rhs_scale=hs[:], start=True, stop=True,
-            )
-            if e < VECTOR_CASTS_FROM:
-                nc.scalar.copy(y_sb[:, e * C : (e + 1) * C], ps[:])
-            else:
-                nc.vector.tensor_copy(y_sb[:, e * C : (e + 1) * C], ps[:])
+            for c0, n in parts(e):
+                hc, hs = h_q[e, c0]
+                ps = psum.tile([P, n], F32, name="y_ps", tag="y_ps", bufs=2)
+                m = slice(e * N, (e + 1) * N)
+                nc.tensor.matmul_mx(
+                    out=ps[:], lhsT=w2_codes[:, m].bitcast(FP8X4), lhsT_scale=w2_scales[:, m],
+                    rhs=hc[:].bitcast(FP8X4), rhs_scale=hs[:], start=True, stop=True,
+                )
+                if e < VY:
+                    nc.scalar.copy(y_sb[:, e * C + c0 : e * C + c0 + n], ps[:])
+                else:
+                    nc.vector.tensor_copy(y_sb[:, e * C + c0 : e * C + c0 + n], ps[:])
 
         for key in planes:
             nc.gpsimd.memset(planes[key][:, T : T + SPARE], 0.0)
@@ -154,55 +199,51 @@ def tile_moe_pre_mlp_silu_kernel(tc, xT, w1, w2, gate, offs, pos1, pos2, pos3, o
         nc.sync.dma_start(offs_sb[:], offs)
         load_plane(0, 0)
         nc.sync.dma_start(out=gate_first[:], in_=gate[0:P, 0:first])
-        load_plane(0, 1)
         load_w1(0, 0)
+        load_plane(0, 1)
         load_plane(0, 2)
-        load_plane(0, 3)
         load_w1(0, 1)
+        load_plane(0, 3)
         load_plane(1, 0)
-        load_plane(1, 1)
         load_w1(1, 0)
+        load_plane(1, 1)
         load_plane(1, 2)
-        load_plane(1, 3)
         load_w1(1, 1)
+        load_plane(1, 3)
         nc.sync.dma_start(out=gate_rest[:], in_=gate[0:P, first:S])
-        for r, pos in enumerate((pos1, pos2, pos3)):
-            nc.sync.dma_start(pos_sb[r][:], pos)
-
         units = [(e0, n, g) for e0, n in BATCHES for g in range(PASSES)]
-
-        def finish(e):
-            layer1(e)
-            if e > 0:
-                layer2(e - 1)
 
         gather(*units[0])
         prepare_w1(0)
-        for u in range(len(units)):
-            e0, n, g = units[u]
-            cast_x(e0, n, g)
-            if g == PASSES - 1:
-                for e in range(e0, e0 + n):
-                    quantize_x(e)
+        for u in range(E + LAG2):
+            if u < len(units):
+                e0, n, g = units[u]
+                cast_x(e0, n, g)
+                if g == PASSES - 1:
+                    for e in range(e0, e0 + n):
+                        quantize_x(e)
             if u + 1 < len(units):
                 gather(*units[u + 1])
-            e = u + 1
-            if e >= 2:
-                load_w1(e, 0)
-                load_w1(e, 1)
-            prepare_w1(e)
-            for e0w, nw in W2_GROUPS:
-                if e0w == u - 1:
-                    load_w2(e0w, nw)
-                    prepare_w2(e0w, nw)
-            if u == len(units) - 1:
-                load_w2(*W2_GROUPS[-1])
-                prepare_w2(*W2_GROUPS[-1])
-            if u >= 1:
-                finish(u - 1)
-        finish(E - 2)
-        finish(E - 1)
-        layer2(E - 1)
+            if 2 <= u + 1 < E:
+                load_w1(u + 1, 0)
+                load_w1(u + 1, 1)
+            for step, widths, e0w, late in W2_GROUPS:
+                if step - W2_LOAD == u:
+                    load_w2(e0w, sum(widths))
+            if u == REST_LOAD:
+                for r, pos in enumerate((pos1, pos2, pos3)):
+                    nc.sync.dma_start(pos_sb[r][:], pos)
+            if u + 1 < E:
+                prepare_w1(u + 1)
+            for step, widths, e0w, late in W2_GROUPS:
+                if step == u:
+                    prepare_w2(widths, e0w, late)
+            if 0 <= u - LAGH < E:
+                quantize_h(u - LAGH)
+            if 0 <= u - LAG1 < E:
+                layer1(u - LAG1)
+            if 0 <= u - LAG2 < E:
+                layer2(u - LAG2)
 
         sums = [keep.tile([P, T], F32, name="sum%d" % r) for r in range(3)]
         for r in range(3):

@@ -23,26 +23,30 @@ PASSES = K // (P * PACK)
 HALF = 128
 SPARE = 16
 BATCHES = [(0, 3), (3, 3), (6, 2), (8, 1)]
-LAG1 = 1
+LAG1 = 2
 LAG2 = 4
 W2_LOAD = 0
 W2_LEAD = 1
 REST_LOAD = 2
 VY = 8
 WB_BUFS = 4
-WQ_BUFS = 8
+WQ_BUFS = 10
 G_BUFS = 2
 H_BUFS = 2
-XB_BUFS = 4
-XQ_BUFS = 4
-RAW_BUFS = 6
+XB_BUFS = 2
+RAW_BUFS = 5
 LATE_TAG = "w_bf"
-W2_GROUPS = [(3, (2, 1), 0, False), (5, (2, 1), 3, False), (7, (2, 1), 6, True)]
-LAGH = 2
-HQ_BUFS = 6
+W2_GROUPS = [(3, (2, 1), 0, False), (6, (2, 1), 3, False), (8, (2, 1), 6, True)]
+LAGH = 3
+HQ_BUFS = 7
 SPLIT = 1
-VSET = (13, 15, 17)
-GSPLIT = 0
+VSET = (11, 13, 15, 17)
+UNITS = [(0, 0), (1, 0), (0, 1), (1, 1), (2, 0), (2, 1), (3, 0), (3, 1)]
+XC_COLS = 768
+XQ_COLS = 512
+XI = 2
+W2_TAG = "raw"
+W2_BUFS = 5
 LATE_BUFS = 4
 PIECES = [[(0, 384), (384, 384)], [(0, 384), (384, 384)], [(0, 384), (384, 256), (640, 128)]]
 
@@ -58,13 +62,14 @@ def tile_moe_pre_mlp_silu_kernel(tc, xT, w1, w2, gate, offs, pos1, pos2, pos3, o
         pos_sb = [keep.tile([P, T // 16], U16, name="pos%d_sb" % r) for r in range(3)]
         planes = {(g, j): keep.tile([P, T + SPARE], F32, name="plane%d%d" % (g, j)) for g in range(PASSES) for j in range(PACK)}
         first = BATCHES[0][1] * C
-        gate_first = keep.tile([P, first], F32, name="gate_first")
-        gate_rest = keep.tile([P, S - first], F32, name="gate_rest")
+        gate_sb = keep.tile([P, S], F32, name="gate_sb")
         y_sb = keep.tile([P, S], F32, name="y_sb")
         w2_codes = keep.tile([P, E * N], U32, name="w2_codes", align_bytes=64)
         w2_scales = keep.tile([P, E * N], U8, name="w2_scales", align_bytes=64)
 
-        w2_raw = {}
+        w2_raw, w2_ready, l2_done = {}, [], set()
+        x_codes = [keep.tile([P, S], U32, name="x_codes%d" % g, align_bytes=64) for g in range(PASSES)]
+        x_scales = [keep.tile([P, S], U8, name="x_scales%d" % g, align_bytes=64) for g in range(PASSES)]
         x_rows = xT.rearrange("(g p j) t -> g j p t", g=PASSES, j=PACK)
         raw, gathered, x_bf, x_q, w_bf, w_q, h_bf, h_ps, h_q = {}, {}, {}, {}, {}, {}, {}, {}, {}
 
@@ -76,33 +81,24 @@ def tile_moe_pre_mlp_silu_kernel(tc, xT, w1, w2, gate, offs, pos1, pos2, pos3, o
             nc.sync.dma_start(out=raw[e, g][:], in_=w1[e, g * 512 : (g + 1) * 512, :].rearrange("(p j) h -> p j h", j=PACK))
 
         def load_w2(e0, n):
-            w2_raw[e0] = ring.tile([P, PACK, n, N], F32, name="w2_raw", tag="raw", bufs=RAW_BUFS)
-            rows = w2.rearrange("e (m t v) n -> v t m e n", t=PACK, v=2)
-            for v in range(2):
-                for t in range(PACK):
-                    nc.sync.dma_start(out=w2_raw[e0][v:P:2, t, :, :], in_=rows[v, t, :, e0 : e0 + n, :])
+            w2_raw[e0] = ring.tile([P, n, PACK * N], F32, name="w2n_raw", tag=W2_TAG, bufs=W2_BUFS)
+            nc.sync.dma_start(out=w2_raw[e0][:], in_=w2[e0 : e0 + n].rearrange("e (p j) n -> p e (j n)", j=PACK))
 
         def gather(e0, n, g):
             t = ring.tile([P, PACK, n * C], F32, name="gathered", tag="gathered", bufs=G_BUFS, align_bytes=64)
             cols = slice(e0 * C // 16, (e0 + n) * C // 16)
-            gates = gate_first[:] if e0 == 0 else gate_rest[:, e0 * C - first : (e0 + n) * C - first]
+            gates = gate_sb[:, e0 * C : (e0 + n) * C]
             for j in range(PACK):
-                if (e0, g, j) == (0, 0, 0) and GSPLIT:
-                    for c0, c1 in ((0, C), (C, first)):
-                        nc.vector.tensor_tensor(
-                            t[:, j, c0:c1], planes[g, j][:].indirect(offs_sb[:, c0 // 16 : c1 // 16]), gate_first[:, c0:c1], MULT)
-                else:
-                    nc.vector.tensor_tensor(t[:, j, :], planes[g, j][:].indirect(offs_sb[:, cols]), gates, MULT)
+                nc.vector.tensor_tensor(t[:, j, :], planes[g, j][:].indirect(offs_sb[:, cols]), gates, MULT)
             gathered[e0, g] = t
 
         def cast_x(e0, n, g):
-            for i in range(n):
-                e = e0 + i
-                if g == 0:
-                    x_bf[e] = ring.tile([P, PASSES, C * PACK], BF16, name="x_bf", tag="x_bf", bufs=XB_BUFS, align_bytes=64)
+            x_bf[e0, g] = ring.tile([P, n * C * PACK], BF16, name="x_bf", tag="x_bf", bufs=XB_BUFS, align_bytes=64)
+            for c0 in range(0, n * C, XC_COLS):
+                c1 = min(c0 + XC_COLS, n * C)
                 nc.scalar.copy(
-                    x_bf[e][:, g, :].rearrange("p (c i j) -> p c j i", i=2, j=PACK),
-                    gathered[e0, g][:, :, i * C : (i + 1) * C].rearrange("p j (c i) -> p c j i", i=2),
+                    x_bf[e0, g][:, c0 * PACK : c1 * PACK].rearrange("p (c i j) -> p c j i", i=XI, j=PACK),
+                    gathered[e0, g][:, :, c0:c1].rearrange("p j (c i) -> p c j i", i=XI),
                 )
 
         def quantize(name, src, width, bufs):
@@ -111,19 +107,25 @@ def tile_moe_pre_mlp_silu_kernel(tc, xT, w1, w2, gate, offs, pos1, pos2, pos3, o
             nc.vector.quantize_mx(out=codes[:].bitcast(FP8X4), scales=scales[:], in_=src)
             return codes, scales
 
-        def quantize_x(e):
-            x_q[e] = quantize("x", x_bf[e][:].rearrange("p g c -> p (g c)"), PASSES * C, XQ_BUFS)
+        def quantize_x(e0, n, g):
+            for c0 in range(0, n * C, XQ_COLS):
+                c1 = min(c0 + XQ_COLS, n * C)
+                cols = slice(e0 * C + c0, e0 * C + c1)
+                nc.vector.quantize_mx(
+                    out=x_codes[g][:, cols].bitcast(FP8X4), scales=x_scales[g][:, cols],
+                    in_=x_bf[e0, g][:, c0 * PACK : c1 * PACK],
+                )
 
         def cast_w1(e, g):
-            src = raw[e, g][:].rearrange("p j (m t v) -> p m t j v", t=PACK, v=2)
+            src = raw[e, g][:].rearrange("p j (m t) -> p m j t", t=PACK)
             if 2 * e + g not in VSET:
                 t = ring.tile([P, PACK * H], BF16, name="w_bf", tag="w_bf", bufs=WB_BUFS, align_bytes=64)
                 w_bf[e, g] = t[:]
-                nc.scalar.copy(w_bf[e, g].rearrange("p (t m v j) -> p m t j v", t=PACK, v=2, j=PACK), src)
+                nc.scalar.copy(w_bf[e, g].rearrange("p (t m j) -> p m j t", t=PACK, j=PACK), src)
             else:
                 t = ring.tile([P, PACK * H], BF16, name="w_bf_late", tag=LATE_TAG, bufs=LATE_BUFS, align_bytes=64)
                 w_bf[e, g] = t[:]
-                nc.vector.tensor_copy(w_bf[e, g].rearrange("p (t m v j) -> p m t j v", t=PACK, v=2, j=PACK), src)
+                nc.vector.tensor_copy(w_bf[e, g].rearrange("p (t m j) -> p m j t", t=PACK, j=PACK), src)
 
         def quantize_w1(e, g):
             w_q[e, g] = quantize("w", w_bf[e, g], H, WQ_BUFS)
@@ -141,8 +143,8 @@ def tile_moe_pre_mlp_silu_kernel(tc, xT, w1, w2, gate, offs, pos1, pos2, pos3, o
             else:
                 t = ring.tile([P, n * N * PACK], BF16, name="w2_bf", tag="w2_bf", bufs=1, align_bytes=64)
             nc.vector.tensor_copy(
-                t[:].rearrange("p (c i j) -> p c j i", i=2, j=PACK),
-                w2_raw[e0][:].rearrange("p j e (c i) -> p (e c) j i", i=2),
+                t[:].rearrange("p (e c i j) -> p e c j i", e=n, i=2, j=PACK),
+                w2_raw[e0][:].rearrange("p e (j c i) -> p e c j i", i=2, j=PACK),
             )
             done = 0
             for width in widths:
@@ -160,9 +162,9 @@ def tile_moe_pre_mlp_silu_kernel(tc, xT, w1, w2, gate, offs, pos1, pos2, pos3, o
                 for t in range(PACK):
                     for g in range(PASSES):
                         wc, ws = w_q[e, g]
-                        xc, xs = x_q[e]
+                        xc, xs = x_codes[g], x_scales[g]
                         m = slice(t * P, (t + 1) * P)
-                        n = slice(g * C + half * HALF, g * C + (half + 1) * HALF)
+                        n = slice(e * C + half * HALF, e * C + (half + 1) * HALF)
                         nc.tensor.matmul_mx(
                             out=ps[:, t, :], lhsT=wc[:, m].bitcast(FP8X4), lhsT_scale=ws[:, m],
                             rhs=xc[:, n].bitcast(FP8X4), rhs_scale=xs[:, n], start=(g == 0), stop=(g == PASSES - 1),
@@ -198,20 +200,22 @@ def tile_moe_pre_mlp_silu_kernel(tc, xT, w1, w2, gate, offs, pos1, pos2, pos3, o
 
         nc.sync.dma_start(offs_sb[:], offs)
         load_plane(0, 0)
-        nc.sync.dma_start(out=gate_first[:], in_=gate[0:P, 0:first])
-        load_w1(0, 0)
+        nc.sync.dma_start(out=gate_sb[:, 0 * C : 3 * C], in_=gate[0:P, 0 * C : 3 * C])
         load_plane(0, 1)
+        load_w1(0, 0)
         load_plane(0, 2)
-        load_w1(0, 1)
         load_plane(0, 3)
-        load_plane(1, 0)
+        load_w1(0, 1)
+        nc.sync.dma_start(out=gate_sb[:, 3 * C : 6 * C], in_=gate[0:P, 3 * C : 6 * C])
         load_w1(1, 0)
-        load_plane(1, 1)
-        load_plane(1, 2)
         load_w1(1, 1)
+        load_plane(1, 0)
+        load_plane(1, 1)
+        load_w1(2, 0)
+        load_plane(1, 2)
         load_plane(1, 3)
-        nc.sync.dma_start(out=gate_rest[:], in_=gate[0:P, first:S])
-        units = [(e0, n, g) for e0, n in BATCHES for g in range(PASSES)]
+        nc.sync.dma_start(out=gate_sb[:, 6 * C : 9 * C], in_=gate[0:P, 6 * C : 9 * C])
+        units = [BATCHES[b] + (g,) for b, g in UNITS]
 
         gather(*units[0])
         prepare_w1(0)
@@ -219,14 +223,13 @@ def tile_moe_pre_mlp_silu_kernel(tc, xT, w1, w2, gate, offs, pos1, pos2, pos3, o
             if u < len(units):
                 e0, n, g = units[u]
                 cast_x(e0, n, g)
-                if g == PASSES - 1:
-                    for e in range(e0, e0 + n):
-                        quantize_x(e)
+                quantize_x(e0, n, g)
             if u + 1 < len(units):
                 gather(*units[u + 1])
-            if 2 <= u + 1 < E:
-                load_w1(u + 1, 0)
-                load_w1(u + 1, 1)
+            if u + 1 < E:
+                for g in range(PASSES):
+                    if (u + 1, g) not in raw:
+                        load_w1(u + 1, g)
             for step, widths, e0w, late in W2_GROUPS:
                 if step - W2_LOAD == u:
                     load_w2(e0w, sum(widths))
@@ -238,12 +241,15 @@ def tile_moe_pre_mlp_silu_kernel(tc, xT, w1, w2, gate, offs, pos1, pos2, pos3, o
             for step, widths, e0w, late in W2_GROUPS:
                 if step == u:
                     prepare_w2(widths, e0w, late)
+                    w2_ready.extend(range(e0w, e0w + sum(widths)))
             if 0 <= u - LAGH < E:
                 quantize_h(u - LAGH)
             if 0 <= u - LAG1 < E:
                 layer1(u - LAG1)
-            if 0 <= u - LAG2 < E:
-                layer2(u - LAG2)
+            for e in range(E):
+                if e not in l2_done and e in w2_ready and u - e >= LAG2:
+                    l2_done.add(e)
+                    layer2(e)
 
         sums = [keep.tile([P, T], F32, name="sum%d" % r) for r in range(3)]
         for r in range(3):

@@ -4,8 +4,9 @@ import concourse.mybir as mybir
 
 K, T, E, C, H, N = 1024, 768, 9, 256, 512, 128
 S = E * C
+TOP = 3
 FLOPS = 2 * S * (K * H + H * N)
-BYTES = 4 * (K * T + E * K * H + E * H * N + S + N * T) + 2 * 128 * (S + 3 * T) // 16
+BYTES = 4 * (K * T + E * K * H + E * H * N + S + N * T) + 2 * 128 * (S + TOP * T) // 16
 
 F32 = mybir.dt.float32
 BF16 = mybir.dt.bfloat16
@@ -19,36 +20,31 @@ SILU = mybir.ActivationFunctionType.Silu
 
 P = 128
 PACK = 4
-PASSES = K // (P * PACK)
+K_PASS = P * PACK
+PASSES = K // K_PASS
+PER_COLUMN = 16
 HALF = 128
+NEIGHBOURS = 2
 SPARE = 16
-BATCHES = [(0, 3), (3, 3), (6, 2), (8, 1)]
-LAG1 = 2
-LAG2 = 4
-W2_LOAD = 0
-W2_LEAD = 1
-REST_LOAD = 2
-VY = 8
-WB_BUFS = 4
-WQ_BUFS = 10
-G_BUFS = 2
-H_BUFS = 2
-XB_BUFS = 2
+
+JOBS = [(0, 3, 0), (3, 3, 0), (0, 3, 1), (3, 3, 1), (6, 2, 0), (6, 2, 1), (8, 1, 0), (8, 1, 1)]
+GATE_PIECE = 3 * C
+X_QUANT = 512
+VECTOR_W1_FROM = 5
+W2_GROUP = 3
+W2_PARTS = [(0, 2), (2, 1)]
+LAG_LAYER1 = 2
+LAG_QUANT_H = 3
+LAG_LAYER2 = 4
+LAG_W2 = 3
+STEP_POS = 2
+COMBINE = [[(0, 384), (384, 384)], [(0, 384), (384, 384)], [(0, 384), (384, 256), (640, 128)]]
+
 RAW_BUFS = 5
-LATE_TAG = "w_bf"
-W2_GROUPS = [(3, (2, 1), 0, False), (6, (2, 1), 3, False), (8, (2, 1), 6, True)]
-LAGH = 3
-HQ_BUFS = 7
-SPLIT = 1
-VSET = (11, 13, 15, 17)
-UNITS = [(0, 0), (1, 0), (0, 1), (1, 1), (2, 0), (2, 1), (3, 0), (3, 1)]
-XC_COLS = 768
-XQ_COLS = 512
-XI = 2
-W2_TAG = "raw"
-W2_BUFS = 5
-LATE_BUFS = 4
-PIECES = [[(0, 384), (384, 384)], [(0, 384), (384, 384)], [(0, 384), (384, 256), (640, 128)]]
+W_BF_BUFS = 4
+W_CODE_BUFS = 10
+H_CODE_BUFS = 7
+A_BANKS, Y_BANKS = 6, 2
 
 
 def tile_moe_pre_mlp_silu_kernel(tc, xT, w1, w2, gate, offs, pos1, pos2, pos3, out):
@@ -58,207 +54,206 @@ def tile_moe_pre_mlp_silu_kernel(tc, xT, w1, w2, gate, offs, pos1, pos2, pos3, o
         ring = ctx.enter_context(tc.tile_pool(name="ring", bufs=2))
         psum = ctx.enter_context(tc.psum_pool(name="psum", bufs=2))
 
-        offs_sb = keep.tile([P, S // 16], U16, name="offs_sb")
-        pos_sb = [keep.tile([P, T // 16], U16, name="pos%d_sb" % r) for r in range(3)]
-        planes = {(g, j): keep.tile([P, T + SPARE], F32, name="plane%d%d" % (g, j)) for g in range(PASSES) for j in range(PACK)}
-        first = BATCHES[0][1] * C
+        offs_sb = keep.tile([P, S // PER_COLUMN], U16, name="offs_sb")
+        pos_sb = [keep.tile([P, T // PER_COLUMN], U16, name="pos%d_sb" % r) for r in range(TOP)]
+        x_rows = {
+            (g, j): keep.tile([P, T + SPARE], F32, name="x_rows%d%d" % (g, j)) for g in range(PASSES) for j in range(PACK)
+        }
         gate_sb = keep.tile([P, S], F32, name="gate_sb")
         y_sb = keep.tile([P, S], F32, name="y_sb")
         w2_codes = keep.tile([P, E * N], U32, name="w2_codes", align_bytes=64)
         w2_scales = keep.tile([P, E * N], U8, name="w2_scales", align_bytes=64)
-
-        w2_raw, w2_ready, l2_done = {}, [], set()
         x_codes = [keep.tile([P, S], U32, name="x_codes%d" % g, align_bytes=64) for g in range(PASSES)]
         x_scales = [keep.tile([P, S], U8, name="x_scales%d" % g, align_bytes=64) for g in range(PASSES)]
-        x_rows = xT.rearrange("(g p j) t -> g j p t", g=PASSES, j=PACK)
-        raw, gathered, x_bf, x_q, w_bf, w_q, h_bf, h_ps, h_q = {}, {}, {}, {}, {}, {}, {}, {}, {}
+        xT_by_word = xT.rearrange("(g p j) t -> g j p t", g=PASSES, j=PACK)
+        w1_raw, w2_raw, gathered, w1_mx, h_bf, h_mx = {}, {}, {}, {}, {}, {}
 
-        def load_plane(g, j):
-            nc.sync.dma_start(out=planes[g, j][:, 0:T], in_=x_rows[g, j])
+        def load_x(g, j):
+            nc.sync.dma_start(out=x_rows[g, j][:, 0:T], in_=xT_by_word[g, j])
+
+        def load_gate(piece):
+            cols = slice(piece * GATE_PIECE, (piece + 1) * GATE_PIECE)
+            nc.sync.dma_start(out=gate_sb[:, cols], in_=gate[0:P, cols])
 
         def load_w1(e, g):
-            raw[e, g] = ring.tile([P, PACK, H], F32, name="raw", tag="raw", bufs=RAW_BUFS)
-            nc.sync.dma_start(out=raw[e, g][:], in_=w1[e, g * 512 : (g + 1) * 512, :].rearrange("(p j) h -> p j h", j=PACK))
+            w1_raw[e, g] = ring.tile([P, PACK, H], F32, name="w1_raw", tag="raw", bufs=RAW_BUFS)
+            rows = w1[e, g * K_PASS : (g + 1) * K_PASS, :]
+            nc.sync.dma_start(out=w1_raw[e, g][:], in_=rows.rearrange("(p j) h -> p j h", j=PACK))
 
-        def load_w2(e0, n):
-            w2_raw[e0] = ring.tile([P, n, PACK * N], F32, name="w2n_raw", tag=W2_TAG, bufs=W2_BUFS)
-            nc.sync.dma_start(out=w2_raw[e0][:], in_=w2[e0 : e0 + n].rearrange("e (p j) n -> p e (j n)", j=PACK))
+        def load_w2(e0):
+            w2_raw[e0] = ring.tile([P, W2_GROUP, PACK * N], F32, name="w2_raw", tag="raw", bufs=RAW_BUFS)
+            group = w2[e0 : e0 + W2_GROUP]
+            nc.sync.dma_start(out=w2_raw[e0][:], in_=group.rearrange("e (p j) n -> p e (j n)", j=PACK))
 
-        def gather(e0, n, g):
-            t = ring.tile([P, PACK, n * C], F32, name="gathered", tag="gathered", bufs=G_BUFS, align_bytes=64)
-            cols = slice(e0 * C // 16, (e0 + n) * C // 16)
-            gates = gate_sb[:, e0 * C : (e0 + n) * C]
+        def gather_x(e0, experts, g):
+            tile = ring.tile([P, PACK, experts * C], F32, name="gathered", tag="gathered", bufs=2, align_bytes=64)
+            entries = offs_sb[:, e0 * C // PER_COLUMN : (e0 + experts) * C // PER_COLUMN]
+            gates = gate_sb[:, e0 * C : (e0 + experts) * C]
             for j in range(PACK):
-                nc.vector.tensor_tensor(t[:, j, :], planes[g, j][:].indirect(offs_sb[:, cols]), gates, MULT)
-            gathered[e0, g] = t
+                nc.vector.tensor_tensor(tile[:, j, :], x_rows[g, j][:].indirect(entries), gates, MULT)
+            gathered[e0, g] = tile
 
-        def cast_x(e0, n, g):
-            x_bf[e0, g] = ring.tile([P, n * C * PACK], BF16, name="x_bf", tag="x_bf", bufs=XB_BUFS, align_bytes=64)
-            for c0 in range(0, n * C, XC_COLS):
-                c1 = min(c0 + XC_COLS, n * C)
-                nc.scalar.copy(
-                    x_bf[e0, g][:, c0 * PACK : c1 * PACK].rearrange("p (c i j) -> p c j i", i=XI, j=PACK),
-                    gathered[e0, g][:, :, c0:c1].rearrange("p j (c i) -> p c j i", i=XI),
-                )
-
-        def quantize(name, src, width, bufs):
-            codes = ring.tile([P, width], U32, name=name + "_codes", tag=name + "_codes", bufs=bufs, align_bytes=64)
-            scales = ring.tile([P, width], U8, name=name + "_scales", tag=name + "_scales", bufs=bufs, align_bytes=64)
-            nc.vector.quantize_mx(out=codes[:].bitcast(FP8X4), scales=scales[:], in_=src)
-            return codes, scales
-
-        def quantize_x(e0, n, g):
-            for c0 in range(0, n * C, XQ_COLS):
-                c1 = min(c0 + XQ_COLS, n * C)
+        def quantize_x(e0, experts, g):
+            slots = experts * C
+            x_bf = ring.tile([P, slots * PACK], BF16, name="x_bf", tag="x_bf", bufs=2, align_bytes=64)
+            nc.scalar.copy(
+                x_bf[:].rearrange("p (c i j) -> p c j i", i=NEIGHBOURS, j=PACK),
+                gathered[e0, g][:].rearrange("p j (c i) -> p c j i", i=NEIGHBOURS),
+            )
+            for c0 in range(0, slots, X_QUANT):
+                c1 = min(c0 + X_QUANT, slots)
                 cols = slice(e0 * C + c0, e0 * C + c1)
                 nc.vector.quantize_mx(
-                    out=x_codes[g][:, cols].bitcast(FP8X4), scales=x_scales[g][:, cols],
-                    in_=x_bf[e0, g][:, c0 * PACK : c1 * PACK],
+                    out=x_codes[g][:, cols].bitcast(FP8X4),
+                    scales=x_scales[g][:, cols],
+                    in_=x_bf[:, c0 * PACK : c1 * PACK],
                 )
 
-        def cast_w1(e, g):
-            src = raw[e, g][:].rearrange("p j (m t) -> p m j t", t=PACK)
-            if 2 * e + g not in VSET:
-                t = ring.tile([P, PACK * H], BF16, name="w_bf", tag="w_bf", bufs=WB_BUFS, align_bytes=64)
-                w_bf[e, g] = t[:]
-                nc.scalar.copy(w_bf[e, g].rearrange("p (t m j) -> p m j t", t=PACK, j=PACK), src)
-            else:
-                t = ring.tile([P, PACK * H], BF16, name="w_bf_late", tag=LATE_TAG, bufs=LATE_BUFS, align_bytes=64)
-                w_bf[e, g] = t[:]
-                nc.vector.tensor_copy(w_bf[e, g].rearrange("p (t m j) -> p m j t", t=PACK, j=PACK), src)
+        def quantize_new(name, values, words, bufs):
+            codes = ring.tile([P, words], U32, name=name + "_codes", tag=name + "_codes", bufs=bufs, align_bytes=64)
+            scales = ring.tile([P, words], U8, name=name + "_scales", tag=name + "_scales", bufs=bufs, align_bytes=64)
+            nc.vector.quantize_mx(out=codes[:].bitcast(FP8X4), scales=scales[:], in_=values)
+            return codes, scales
 
-        def quantize_w1(e, g):
-            w_q[e, g] = quantize("w", w_bf[e, g], H, WQ_BUFS)
-
-        def prepare_w1(e):
+        def quantize_w1(e):
+            rounded = []
             for g in range(PASSES):
-                cast_w1(e, g)
+                w_bf = ring.tile([P, PACK * H], BF16, name="w_bf", tag="w_bf", bufs=W_BF_BUFS, align_bytes=64)
+                on_vector = e >= VECTOR_W1_FROM and g == PASSES - 1
+                (nc.vector.tensor_copy if on_vector else nc.scalar.copy)(
+                    w_bf[:].rearrange("p (t m j) -> p m j t", t=PACK, j=PACK),
+                    w1_raw[e, g][:].rearrange("p j (m t) -> p m j t", t=PACK),
+                )
+                rounded.append(w_bf)
             for g in range(PASSES):
-                quantize_w1(e, g)
+                w1_mx[e, g] = quantize_new("w", rounded[g][:], H, W_CODE_BUFS)
 
-        def prepare_w2(widths, e0, late):
-            n = sum(widths)
-            if late:
-                t = ring.tile([P, n * N * PACK], BF16, name="w2_bf", tag=LATE_TAG, bufs=LATE_BUFS, align_bytes=64)
+        def quantize_w2(e0):
+            if e0 + W2_GROUP < E:
+                w2_bf = ring.tile([P, W2_GROUP * N * PACK], BF16, name="w2_bf", tag="w2_bf", bufs=1, align_bytes=64)
             else:
-                t = ring.tile([P, n * N * PACK], BF16, name="w2_bf", tag="w2_bf", bufs=1, align_bytes=64)
-            nc.vector.tensor_copy(
-                t[:].rearrange("p (e c i j) -> p e c j i", e=n, i=2, j=PACK),
-                w2_raw[e0][:].rearrange("p e (j c i) -> p e c j i", i=2, j=PACK),
-            )
-            done = 0
-            for width in widths:
-                cols = slice((e0 + done) * N, (e0 + done + width) * N)
+                w2_bf = ring.tile([P, W2_GROUP * N * PACK], BF16, name="w2_bf", tag="w_bf", bufs=W_BF_BUFS, align_bytes=64)
+            for i0, experts in W2_PARTS:
+                nc.vector.tensor_copy(
+                    w2_bf[:, i0 * N * PACK : (i0 + experts) * N * PACK].rearrange(
+                        "p (e c i j) -> p e c j i", e=experts, i=NEIGHBOURS, j=PACK
+                    ),
+                    w2_raw[e0][:, i0 : i0 + experts, :].rearrange("p e (j c i) -> p e c j i", i=NEIGHBOURS, j=PACK),
+                )
+            for i0, experts in W2_PARTS:
+                cols = slice((e0 + i0) * N, (e0 + i0 + experts) * N)
                 nc.vector.quantize_mx(
-                    out=w2_codes[:, cols].bitcast(FP8X4), scales=w2_scales[:, cols],
-                    in_=t[:, done * N * PACK : (done + width) * N * PACK],
+                    out=w2_codes[:, cols].bitcast(FP8X4),
+                    scales=w2_scales[:, cols],
+                    in_=w2_bf[:, i0 * N * PACK : (i0 + experts) * N * PACK],
                 )
-                done = done + width
 
         def layer1(e):
-            h_bf[e] = ring.tile([P, C * PACK], BF16, name="h_bf", tag="h_bf", bufs=H_BUFS, align_bytes=64)
-            for half in range(C // HALF):
-                ps = psum.tile([P, PACK, HALF], F32, name="a_ps", tag="a_ps", bufs=6)
+            h_bf[e] = ring.tile([P, C * PACK], BF16, name="h_bf", tag="h_bf", bufs=2, align_bytes=64)
+            for c0 in range(0, C, HALF):
+                a_ps = psum.tile([P, PACK, HALF], F32, name="a_ps", tag="a_ps", bufs=A_BANKS)
+                slots = slice(e * C + c0, e * C + c0 + HALF)
                 for t in range(PACK):
+                    channels = slice(t * P, (t + 1) * P)
                     for g in range(PASSES):
-                        wc, ws = w_q[e, g]
-                        xc, xs = x_codes[g], x_scales[g]
-                        m = slice(t * P, (t + 1) * P)
-                        n = slice(e * C + half * HALF, e * C + (half + 1) * HALF)
+                        codes, scales = w1_mx[e, g]
                         nc.tensor.matmul_mx(
-                            out=ps[:, t, :], lhsT=wc[:, m].bitcast(FP8X4), lhsT_scale=ws[:, m],
-                            rhs=xc[:, n].bitcast(FP8X4), rhs_scale=xs[:, n], start=(g == 0), stop=(g == PASSES - 1),
+                            out=a_ps[:, t, :],
+                            lhsT=codes[:, channels].bitcast(FP8X4),
+                            lhsT_scale=scales[:, channels],
+                            rhs=x_codes[g][:, slots].bitcast(FP8X4),
+                            rhs_scale=x_scales[g][:, slots],
+                            start=(g == 0),
+                            stop=(g == PASSES - 1),
                         )
                 nc.scalar.activation(
-                    h_bf[e][:, half * 512 : (half + 1) * 512].rearrange("p (n t) -> p n t", t=PACK),
-                    ps[:].rearrange("p t n -> p n t"), SILU,
+                    h_bf[e][:, c0 * PACK : (c0 + HALF) * PACK].rearrange("p (n t) -> p n t", t=PACK),
+                    a_ps[:].rearrange("p t n -> p n t"),
+                    SILU,
                 )
 
-        def parts(e):
-            return [(0, C)] if e < E - SPLIT else [(0, HALF), (HALF, HALF)]
+        def slot_ranges(e):
+            return [(0, C)] if e < E - 1 else [(0, HALF), (HALF, HALF)]
 
         def quantize_h(e):
-            for c0, n in parts(e):
-                h_q[e, c0] = quantize("h", h_bf[e][:, c0 * PACK : (c0 + n) * PACK], n, HQ_BUFS)
+            for c0, slots in slot_ranges(e):
+                h_mx[e, c0] = quantize_new("h", h_bf[e][:, c0 * PACK : (c0 + slots) * PACK], slots, H_CODE_BUFS)
 
         def layer2(e):
-            for c0, n in parts(e):
-                hc, hs = h_q[e, c0]
-                ps = psum.tile([P, n], F32, name="y_ps", tag="y_ps", bufs=2)
-                m = slice(e * N, (e + 1) * N)
+            for c0, slots in slot_ranges(e):
+                codes, scales = h_mx[e, c0]
+                y_ps = psum.tile([P, slots], F32, name="y_ps", tag="y_ps", bufs=Y_BANKS)
+                cols = slice(e * N, (e + 1) * N)
                 nc.tensor.matmul_mx(
-                    out=ps[:], lhsT=w2_codes[:, m].bitcast(FP8X4), lhsT_scale=w2_scales[:, m],
-                    rhs=hc[:].bitcast(FP8X4), rhs_scale=hs[:], start=True, stop=True,
+                    out=y_ps[:],
+                    lhsT=w2_codes[:, cols].bitcast(FP8X4),
+                    lhsT_scale=w2_scales[:, cols],
+                    rhs=codes[:].bitcast(FP8X4),
+                    rhs_scale=scales[:],
+                    start=True,
+                    stop=True,
                 )
-                if e < VY:
-                    nc.scalar.copy(y_sb[:, e * C + c0 : e * C + c0 + n], ps[:])
-                else:
-                    nc.vector.tensor_copy(y_sb[:, e * C + c0 : e * C + c0 + n], ps[:])
+                (nc.scalar.copy if e < E - 1 else nc.vector.tensor_copy)(
+                    y_sb[:, e * C + c0 : e * C + c0 + slots], y_ps[:]
+                )
 
-        for key in planes:
-            nc.gpsimd.memset(planes[key][:, T : T + SPARE], 0.0)
+        for key in x_rows:
+            nc.gpsimd.memset(x_rows[key][:, T : T + SPARE], 0.0)
 
         nc.sync.dma_start(offs_sb[:], offs)
-        load_plane(0, 0)
-        nc.sync.dma_start(out=gate_sb[:, 0 * C : 3 * C], in_=gate[0:P, 0 * C : 3 * C])
-        load_plane(0, 1)
+        load_x(0, 0)
+        load_gate(0)
+        load_x(0, 1)
         load_w1(0, 0)
-        load_plane(0, 2)
-        load_plane(0, 3)
+        load_x(0, 2)
+        load_x(0, 3)
         load_w1(0, 1)
-        nc.sync.dma_start(out=gate_sb[:, 3 * C : 6 * C], in_=gate[0:P, 3 * C : 6 * C])
+        load_gate(1)
         load_w1(1, 0)
         load_w1(1, 1)
-        load_plane(1, 0)
-        load_plane(1, 1)
+        load_x(1, 0)
+        load_x(1, 1)
         load_w1(2, 0)
-        load_plane(1, 2)
-        load_plane(1, 3)
-        nc.sync.dma_start(out=gate_sb[:, 6 * C : 9 * C], in_=gate[0:P, 6 * C : 9 * C])
-        units = [BATCHES[b] + (g,) for b, g in UNITS]
+        load_x(1, 2)
+        load_x(1, 3)
+        load_gate(2)
 
-        gather(*units[0])
-        prepare_w1(0)
-        for u in range(E + LAG2):
-            if u < len(units):
-                e0, n, g = units[u]
-                cast_x(e0, n, g)
-                quantize_x(e0, n, g)
-            if u + 1 < len(units):
-                gather(*units[u + 1])
-            if u + 1 < E:
+        w2_step = {min(e0 + LAG_W2, E - 1): e0 for e0 in range(0, E, W2_GROUP)}
+        gather_x(*JOBS[0])
+        quantize_w1(0)
+        for step in range(E + LAG_LAYER2):
+            if step < len(JOBS):
+                quantize_x(*JOBS[step])
+            if step + 1 < len(JOBS):
+                gather_x(*JOBS[step + 1])
+            if step + 1 < E:
                 for g in range(PASSES):
-                    if (u + 1, g) not in raw:
-                        load_w1(u + 1, g)
-            for step, widths, e0w, late in W2_GROUPS:
-                if step - W2_LOAD == u:
-                    load_w2(e0w, sum(widths))
-            if u == REST_LOAD:
+                    if (step + 1, g) not in w1_raw:
+                        load_w1(step + 1, g)
+            if step in w2_step:
+                load_w2(w2_step[step])
+            if step == STEP_POS:
                 for r, pos in enumerate((pos1, pos2, pos3)):
                     nc.sync.dma_start(pos_sb[r][:], pos)
-            if u + 1 < E:
-                prepare_w1(u + 1)
-            for step, widths, e0w, late in W2_GROUPS:
-                if step == u:
-                    prepare_w2(widths, e0w, late)
-                    w2_ready.extend(range(e0w, e0w + sum(widths)))
-            if 0 <= u - LAGH < E:
-                quantize_h(u - LAGH)
-            if 0 <= u - LAG1 < E:
-                layer1(u - LAG1)
-            for e in range(E):
-                if e not in l2_done and e in w2_ready and u - e >= LAG2:
-                    l2_done.add(e)
-                    layer2(e)
+            if step + 1 < E:
+                quantize_w1(step + 1)
+            if step in w2_step:
+                quantize_w2(w2_step[step])
+            if 0 <= step - LAG_QUANT_H < E:
+                quantize_h(step - LAG_QUANT_H)
+            if 0 <= step - LAG_LAYER1 < E:
+                layer1(step - LAG_LAYER1)
+            if 0 <= step - LAG_LAYER2 < E:
+                layer2(step - LAG_LAYER2)
 
-        sums = [keep.tile([P, T], F32, name="sum%d" % r) for r in range(3)]
-        for r in range(3):
-            for i, (t0, n) in enumerate(PIECES[r]):
-                cols = slice(t0, t0 + n)
-                picked = y_sb[:].indirect(pos_sb[r][:, t0 // 16 : (t0 + n) // 16])
+        sums = [keep.tile([P, T], F32, name="sum%d" % r) for r in range(TOP)]
+        for r in range(TOP):
+            for i, (t0, tokens) in enumerate(COMBINE[r]):
+                cols = slice(t0, t0 + tokens)
+                picked = y_sb[:].indirect(pos_sb[r][:, t0 // PER_COLUMN : (t0 + tokens) // PER_COLUMN])
                 if r == 0:
                     nc.vector.tensor_copy(sums[r][:, cols], picked)
                 else:
                     nc.vector.tensor_tensor(sums[r][:, cols], picked, sums[r - 1][:, cols], ADD)
-                if r == 2:
+                if r == TOP - 1:
                     (nc.sync if i % 2 == 0 else nc.scalar).dma_start(out=out[:, cols], in_=sums[r][:, cols])

from contextlib import ExitStack

import concourse.mybir as mybir

K, T, E, C, H, N = 1024, 768, 9, 256, 512, 128
S = E * C
TOP = 3
FLOPS = 2 * S * (K * H + H * N)
BYTES = 4 * (K * T + E * K * H + E * H * N + S + N * T) + 2 * 128 * (S + TOP * T) // 16

F32 = mybir.dt.float32
BF16 = mybir.dt.bfloat16
U32 = mybir.dt.uint32
U16 = mybir.dt.uint16
U8 = mybir.dt.uint8
FP8X4 = mybir.dt.float8_e4m3fn_x4
MULT = mybir.AluOpType.mult
ADD = mybir.AluOpType.add
SILU = mybir.ActivationFunctionType.Silu

P = 128
PACK = 4
K_PASS = P * PACK
PASSES = K // K_PASS
PER_COLUMN = 16
HALF = 128
NEIGHBOURS = 2
SPARE = 16

JOBS = [(0, 3, 0), (3, 3, 0), (0, 3, 1), (3, 3, 1), (6, 2, 0), (6, 2, 1), (8, 1, 0), (8, 1, 1)]
GATE_PIECE = 3 * C
X_QUANT = 512
VECTOR_W1_FROM = 5
W2_GROUP = 3
W2_PARTS = [(0, 2), (2, 1)]
LAG_LAYER1 = 2
LAG_QUANT_H = 3
LAG_LAYER2 = 4
LAG_W2 = 3
STEP_POS = 2
COMBINE = [[(0, 384), (384, 384)], [(0, 384), (384, 384)], [(0, 384), (384, 256), (640, 128)]]

RAW_BUFS = 5
W_BF_BUFS = 4
W_CODE_BUFS = 10
H_CODE_BUFS = 7
A_BANKS, Y_BANKS = 6, 2


def tile_moe_pre_mlp_silu_kernel(tc, xT, w1, w2, gate, offs, pos1, pos2, pos3, out):
    nc = tc.nc
    with ExitStack() as ctx:
        keep = ctx.enter_context(tc.tile_pool(name="keep", bufs=1))
        ring = ctx.enter_context(tc.tile_pool(name="ring", bufs=2))
        psum = ctx.enter_context(tc.psum_pool(name="psum", bufs=2))

        offs_sb = keep.tile([P, S // PER_COLUMN], U16, name="offs_sb")
        pos_sb = [keep.tile([P, T // PER_COLUMN], U16, name="pos%d_sb" % r) for r in range(TOP)]
        x_rows = {
            (g, j): keep.tile([P, T + SPARE], F32, name="x_rows%d%d" % (g, j)) for g in range(PASSES) for j in range(PACK)
        }
        gate_sb = keep.tile([P, S], F32, name="gate_sb")
        y_sb = keep.tile([P, S], F32, name="y_sb")
        w2_codes = keep.tile([P, E * N], U32, name="w2_codes", align_bytes=64)
        w2_scales = keep.tile([P, E * N], U8, name="w2_scales", align_bytes=64)
        x_codes = [keep.tile([P, S], U32, name="x_codes%d" % g, align_bytes=64) for g in range(PASSES)]
        x_scales = [keep.tile([P, S], U8, name="x_scales%d" % g, align_bytes=64) for g in range(PASSES)]
        xT_by_word = xT.rearrange("(g p j) t -> g j p t", g=PASSES, j=PACK)
        w1_raw, w2_raw, gathered, w1_mx, h_bf, h_mx = {}, {}, {}, {}, {}, {}

        def load_x(g, j):
            nc.sync.dma_start(out=x_rows[g, j][:, 0:T], in_=xT_by_word[g, j])

        def load_gate(piece):
            cols = slice(piece * GATE_PIECE, (piece + 1) * GATE_PIECE)
            nc.sync.dma_start(out=gate_sb[:, cols], in_=gate[0:P, cols])

        def load_w1(e, g):
            w1_raw[e, g] = ring.tile([P, PACK, H], F32, name="w1_raw", tag="raw", bufs=RAW_BUFS)
            rows = w1[e, g * K_PASS : (g + 1) * K_PASS, :]
            nc.sync.dma_start(out=w1_raw[e, g][:], in_=rows.rearrange("(p j) h -> p j h", j=PACK))

        def load_w2(e0):
            w2_raw[e0] = ring.tile([P, W2_GROUP, PACK * N], F32, name="w2_raw", tag="raw", bufs=RAW_BUFS)
            group = w2[e0 : e0 + W2_GROUP]
            nc.sync.dma_start(out=w2_raw[e0][:], in_=group.rearrange("e (p j) n -> p e (j n)", j=PACK))

        def gather_x(e0, experts, g):
            tile = ring.tile([P, PACK, experts * C], F32, name="gathered", tag="gathered", bufs=2, align_bytes=64)
            entries = offs_sb[:, e0 * C // PER_COLUMN : (e0 + experts) * C // PER_COLUMN]
            gates = gate_sb[:, e0 * C : (e0 + experts) * C]
            for j in range(PACK):
                nc.vector.tensor_tensor(tile[:, j, :], x_rows[g, j][:].indirect(entries), gates, MULT)
            gathered[e0, g] = tile

        def quantize_x(e0, experts, g):
            slots = experts * C
            x_bf = ring.tile([P, slots * PACK], BF16, name="x_bf", tag="x_bf", bufs=2, align_bytes=64)
            nc.scalar.copy(
                x_bf[:].rearrange("p (c i j) -> p c j i", i=NEIGHBOURS, j=PACK),
                gathered[e0, g][:].rearrange("p j (c i) -> p c j i", i=NEIGHBOURS),
            )
            for c0 in range(0, slots, X_QUANT):
                c1 = min(c0 + X_QUANT, slots)
                cols = slice(e0 * C + c0, e0 * C + c1)
                nc.vector.quantize_mx(
                    out=x_codes[g][:, cols].bitcast(FP8X4),
                    scales=x_scales[g][:, cols],
                    in_=x_bf[:, c0 * PACK : c1 * PACK],
                )

        def quantize_new(name, values, words, bufs):
            codes = ring.tile([P, words], U32, name=name + "_codes", tag=name + "_codes", bufs=bufs, align_bytes=64)
            scales = ring.tile([P, words], U8, name=name + "_scales", tag=name + "_scales", bufs=bufs, align_bytes=64)
            nc.vector.quantize_mx(out=codes[:].bitcast(FP8X4), scales=scales[:], in_=values)
            return codes, scales

        def quantize_w1(e):
            rounded = []
            for g in range(PASSES):
                w_bf = ring.tile([P, PACK * H], BF16, name="w_bf", tag="w_bf", bufs=W_BF_BUFS, align_bytes=64)
                on_vector = e >= VECTOR_W1_FROM and g == PASSES - 1
                (nc.vector.tensor_copy if on_vector else nc.scalar.copy)(
                    w_bf[:].rearrange("p (t m j) -> p m j t", t=PACK, j=PACK),
                    w1_raw[e, g][:].rearrange("p j (m t) -> p m j t", t=PACK),
                )
                rounded.append(w_bf)
            for g in range(PASSES):
                w1_mx[e, g] = quantize_new("w", rounded[g][:], H, W_CODE_BUFS)

        def quantize_w2(e0):
            if e0 + W2_GROUP < E:
                w2_bf = ring.tile([P, W2_GROUP * N * PACK], BF16, name="w2_bf", tag="w2_bf", bufs=1, align_bytes=64)
            else:
                w2_bf = ring.tile([P, W2_GROUP * N * PACK], BF16, name="w2_bf", tag="w_bf", bufs=W_BF_BUFS, align_bytes=64)
            for i0, experts in W2_PARTS:
                nc.vector.tensor_copy(
                    w2_bf[:, i0 * N * PACK : (i0 + experts) * N * PACK].rearrange(
                        "p (e c i j) -> p e c j i", e=experts, i=NEIGHBOURS, j=PACK
                    ),
                    w2_raw[e0][:, i0 : i0 + experts, :].rearrange("p e (j c i) -> p e c j i", i=NEIGHBOURS, j=PACK),
                )
            for i0, experts in W2_PARTS:
                cols = slice((e0 + i0) * N, (e0 + i0 + experts) * N)
                nc.vector.quantize_mx(
                    out=w2_codes[:, cols].bitcast(FP8X4),
                    scales=w2_scales[:, cols],
                    in_=w2_bf[:, i0 * N * PACK : (i0 + experts) * N * PACK],
                )

        def layer1(e):
            h_bf[e] = ring.tile([P, C * PACK], BF16, name="h_bf", tag="h_bf", bufs=2, align_bytes=64)
            for c0 in range(0, C, HALF):
                a_ps = psum.tile([P, PACK, HALF], F32, name="a_ps", tag="a_ps", bufs=A_BANKS)
                slots = slice(e * C + c0, e * C + c0 + HALF)
                for t in range(PACK):
                    channels = slice(t * P, (t + 1) * P)
                    for g in range(PASSES):
                        codes, scales = w1_mx[e, g]
                        nc.tensor.matmul_mx(
                            out=a_ps[:, t, :],
                            lhsT=codes[:, channels].bitcast(FP8X4),
                            lhsT_scale=scales[:, channels],
                            rhs=x_codes[g][:, slots].bitcast(FP8X4),
                            rhs_scale=x_scales[g][:, slots],
                            start=(g == 0),
                            stop=(g == PASSES - 1),
                        )
                nc.scalar.activation(
                    h_bf[e][:, c0 * PACK : (c0 + HALF) * PACK].rearrange("p (n t) -> p n t", t=PACK),
                    a_ps[:].rearrange("p t n -> p n t"),
                    SILU,
                )

        def slot_ranges(e):
            return [(0, C)] if e < E - 1 else [(0, HALF), (HALF, HALF)]

        def quantize_h(e):
            for c0, slots in slot_ranges(e):
                h_mx[e, c0] = quantize_new("h", h_bf[e][:, c0 * PACK : (c0 + slots) * PACK], slots, H_CODE_BUFS)

        def layer2(e):
            for c0, slots in slot_ranges(e):
                codes, scales = h_mx[e, c0]
                y_ps = psum.tile([P, slots], F32, name="y_ps", tag="y_ps", bufs=Y_BANKS)
                cols = slice(e * N, (e + 1) * N)
                nc.tensor.matmul_mx(
                    out=y_ps[:],
                    lhsT=w2_codes[:, cols].bitcast(FP8X4),
                    lhsT_scale=w2_scales[:, cols],
                    rhs=codes[:].bitcast(FP8X4),
                    rhs_scale=scales[:],
                    start=True,
                    stop=True,
                )
                (nc.scalar.copy if e < E - 1 else nc.vector.tensor_copy)(
                    y_sb[:, e * C + c0 : e * C + c0 + slots], y_ps[:]
                )

        for key in x_rows:
            nc.gpsimd.memset(x_rows[key][:, T : T + SPARE], 0.0)

        nc.sync.dma_start(offs_sb[:], offs)
        load_x(0, 0)
        load_gate(0)
        load_x(0, 1)
        load_w1(0, 0)
        load_x(0, 2)
        load_x(0, 3)
        load_w1(0, 1)
        load_gate(1)
        load_w1(1, 0)
        load_w1(1, 1)
        load_x(1, 0)
        load_x(1, 1)
        load_w1(2, 0)
        load_x(1, 2)
        load_x(1, 3)
        load_gate(2)

        w2_step = {min(e0 + LAG_W2, E - 1): e0 for e0 in range(0, E, W2_GROUP)}
        gather_x(*JOBS[0])
        quantize_w1(0)
        for step in range(E + LAG_LAYER2):
            if step < len(JOBS):
                quantize_x(*JOBS[step])
            if step + 1 < len(JOBS):
                gather_x(*JOBS[step + 1])
            if step + 1 < E:
                for g in range(PASSES):
                    if (step + 1, g) not in w1_raw:
                        load_w1(step + 1, g)
            if step in w2_step:
                load_w2(w2_step[step])
            if step == STEP_POS:
                for r, pos in enumerate((pos1, pos2, pos3)):
                    nc.sync.dma_start(pos_sb[r][:], pos)
            if step + 1 < E:
                quantize_w1(step + 1)
            if step in w2_step:
                quantize_w2(w2_step[step])
            if 0 <= step - LAG_QUANT_H < E:
                quantize_h(step - LAG_QUANT_H)
            if 0 <= step - LAG_LAYER1 < E:
                layer1(step - LAG_LAYER1)
            if 0 <= step - LAG_LAYER2 < E:
                layer2(step - LAG_LAYER2)

        sums = [keep.tile([P, T], F32, name="sum%d" % r) for r in range(TOP)]
        for r in range(TOP):
            for i, (t0, tokens) in enumerate(COMBINE[r]):
                cols = slice(t0, t0 + tokens)
                picked = y_sb[:].indirect(pos_sb[r][:, t0 // PER_COLUMN : (t0 + tokens) // PER_COLUMN])
                if r == 0:
                    nc.vector.tensor_copy(sums[r][:, cols], picked)
                else:
                    nc.vector.tensor_tensor(sums[r][:, cols], picked, sums[r - 1][:, cols], ADD)
                if r == TOP - 1:
                    (nc.sync if i % 2 == 0 else nc.scalar).dma_start(out=out[:, cols], in_=sums[r][:, cols])
